import numpy as np
import ml_dtypes


def mxq(x, axis, fmt="e4m3"):
    dtype, down = {"e4m3": (ml_dtypes.float8_e4m3fn, 7), "e5m2": (ml_dtypes.float8_e5m2, 14)}[fmt]
    v = np.moveaxis(np.asarray(x, np.float32).astype(ml_dtypes.bfloat16).astype(np.float64), axis, -1)
    blocks = v.reshape(v.shape[:-1] + (-1, 32))
    amax = np.abs(blocks).max(-1, keepdims=True)
    byte = np.maximum(np.where(amax > 0, np.frexp(amax)[1] - 1 + 127, 0) - down, 1)
    scale = np.exp2(byte - 127.0)
    codes = (blocks / scale).astype(np.float32).astype(dtype).astype(np.float64)
    return np.moveaxis((codes * scale).reshape(v.shape), -1, axis)


WIDE = False


def mx_kscale(k):
    if not WIDE:
        return np.ones(k)
    levels = np.array([10, -10, 5, -5, 0])
    if k % 512:
        return np.exp2(np.random.permutation(np.resize(levels, k // 32))).repeat(32)
    a = np.empty((k // 512, 16))
    for p in range(k // 512):
        a[p, :8] = np.random.permutation(np.resize(levels, 8))
        for g in range(8):
            far = levels[np.abs(levels - a[p, g]) >= 10]
            a[p, g + 8] = far[np.random.randint(len(far))]
    return np.exp2(a.ravel()).repeat(32)


def f64(x):
    return np.asarray(x).astype(np.float64)


def striped(idx):
    return np.tile(idx.reshape(-1, 16).T, (8, 1)).astype(np.uint16)


def unstriped(offs):
    return offs[:16].T.reshape(-1).astype(np.int64)


E2M1 = np.array([0.0, 0.5, 1.0, 1.5, 2.0, 3.0, 4.0, 6.0, -0.0, -0.5, -1.0, -1.5, -2.0, -3.0, -4.0, -6.0])


def pack_weight(w, fmt):
    k, n = w.shape
    w = f64(np.asarray(w, np.float32).astype(ml_dtypes.bfloat16)).reshape(k // 32, 32, n)
    amax = np.abs(w).max(1)
    if fmt == "e4m3":
        byte = np.frexp(amax)[1] - 1 + 127 - 7
    else:
        mant, ex = np.frexp(amax / 6.0)
        byte = np.where(mant > 0.5, ex, ex - 1) + 127
    byte = np.clip(np.where(amax > 0, byte, 1), 1, 254)
    scaled = (w * np.exp2(127.0 - byte)[:, None, :]).reshape(k, n).astype(np.float32)
    by_word = np.ascontiguousarray(scaled.reshape(k // 512, 128, 4, n).transpose(0, 1, 3, 2))
    if fmt == "e4m3":
        words = by_word.astype(ml_dtypes.float8_e4m3fn).view(np.uint8)
    else:
        c = by_word.astype(ml_dtypes.float4_e2m1fn).view(np.uint8) & 0xF
        words = (c[..., 0::2] | (c[..., 1::2] << 4)).reshape(k // 512, 128, 2 * n)
    return np.ascontiguousarray(words), np.ascontiguousarray(byte.astype(np.uint8).reshape(k // 512, 16, n))


def unpack_weight(words, scales, fmt):
    g, _, n = scales.shape
    words = np.ascontiguousarray(words).reshape(g, 128, n, -1)
    if fmt == "e4m3":
        vals = words.view(ml_dtypes.float8_e4m3fn).astype(np.float64)
    else:
        nib = np.empty((g, 128, n, 4), np.uint8)
        nib[..., 0::2] = words & 0xF
        nib[..., 1::2] = words >> 4
        vals = E2M1[nib]
    vals = vals * np.repeat(np.exp2(scales.astype(np.float64) - 127.0), 8, axis=1)[..., None]
    return vals.transpose(0, 1, 3, 2).reshape(g * 512, n)


def gelu(v):
    return 0.5 * v * (1.0 + np.tanh(np.sqrt(2.0 / np.pi) * (v + 0.044715 * v**3)))


def bf(x):
    return np.asarray(x, np.float32).astype(ml_dtypes.bfloat16)


def planes(Y):
    n, m = Y.shape
    b = f64(bf(Y)).reshape(n // 32, 32, m)
    amax = np.abs(b).max(1)
    byte = np.clip(np.where(amax > 0, np.frexp(amax)[1] - 1 + 127 - 7, 1), 1, 254)
    codes = (b * np.exp2(127.0 - byte)[:, None, :]).reshape(n, m).astype(np.float32).astype(ml_dtypes.float8_e4m3fn).view(np.uint8)
    words = codes.reshape(n // 512, 128, 4, m).transpose(0, 1, 3, 2)
    return np.ascontiguousarray(words), np.ascontiguousarray(byte.astype(np.uint8).reshape(n // 512, 16, m))


K, H, N, T, S, P = 1024, 1024, 512, 4096, 1024, 512


def setup_inputs():
    n = np.random.standard_normal
    s = mx_kscale(K)[:, None]
    u = mx_kscale(H)[:, None]
    size = np.exp(0.8 * n(N))[None, :]
    d = {}
    d["tab_words"], d["tab_scales"] = pack_weight(n((K, T)) * s, "e4m3")
    d["offs"] = striped(np.random.permutation(T)[:S])
    d["w1"] = (3.0 * n((K, H)) / K ** 0.5 / s).astype(np.float32)
    d["gain"] = (np.exp(0.3 * n(H)) * u[:, 0]).astype(np.float32)
    d["w2_words"], d["w2_scales"] = pack_weight(1.2 * n((H, N)) / H ** 0.5 / u * size, "e2m1")
    d["w3_words"], d["w3_scales"] = pack_weight(1.4 * n((K, N)) / K ** 0.5 / s * size, "e4m3")
    d["pos1"] = striped(np.random.permutation(S)[:P])
    d["pos2"] = striped(np.random.permutation(S)[:P])
    d["gx"] = (0.6 * np.exp(0.3 * n(N))).astype(np.float32)
    return d


def reference(tab_words, tab_scales, offs, w1, gain, w2_words, w2_scales,
              w3_words, w3_scales, pos1, pos2, gx):
    v = unpack_weight(tab_words, tab_scales, "e4m3")[:, unstriped(offs)]
    w2 = unpack_weight(w2_words, w2_scales, "e2m1")
    w3 = unpack_weight(w3_words, w3_scales, "e4m3")
    x = mxq(f64(w1), 0, "e4m3").T @ v
    h = np.log(1.0 + np.abs(x)) * f64(gain)[:, None]
    a = w2.T @ mxq(h, 0, "e4m3")
    b = w3.T @ v
    g2 = np.minimum(a, b)
    y = g2[:, unstriped(pos1)] - f64(gx)[:, None] * g2[:, unstriped(pos2)]
    words, scales = planes(y)
    return y, words, scales

@@ -1,0 +1,285 @@
+from contextlib import ExitStack
+
+import concourse.mybir as mybir
+
+K, H, N, T, S, PAIRS = 1024, 1024, 512, 4096, 1024, 512
+FLOPS = 2 * S * (K * H + H * N + K * N)
+
+F32 = mybir.dt.float32
+BF16 = mybir.dt.bfloat16
+I32 = mybir.dt.int32
+U32 = mybir.dt.uint32
+U16 = mybir.dt.uint16
+U8 = mybir.dt.uint8
+FP8X4 = mybir.dt.float8_e4m3fn_x4
+FP4X4 = mybir.dt.float4_e2m1fn_x4
+ACT = mybir.ActivationFunctionType
+ALU = mybir.AluOpType
+
+P = 128
+PACK = 4
+PASS = P * PACK
+PASSES = 2
+BANK = 512
+X_COLS = BANK // PACK
+STEP = 256
+PAIR_SLICES = (256, 128, 128)
+
+
+def tile_list_coil_pair_traces_kernel(
+    tc, tab_words, tab_scales, offs, w1, gain, w2_words, w2_scales, w3_words, w3_scales, pos1, pos2, gx,
+    out_0, out_1, out_2,
+):
+    nc = tc.nc
+    with ExitStack() as ctx:
+        keep = ctx.enter_context(tc.tile_pool(name="keep", bufs=1))
+        ring = ctx.enter_context(tc.tile_pool(name="ring", bufs=3))
+        psum = ctx.enter_context(tc.psum_pool(name="psum", bufs=8))
+
+        def kept(name, shape, dtype, tag=None):
+            return keep.tile(shape, dtype, name=name, tag=tag or name, align_bytes=64)
+
+        offs_sb = keep.tile([P, S // 16], U16, name="offs_sb")
+        pos1_sb = keep.tile([P, PAIRS // 16], U16, name="pos1_sb")
+        pos2_sb = keep.tile([P, PAIRS // 16], U16, name="pos2_sb")
+
+        tab_sc = kept("tab_sc", [P, T], U8, "stage01")
+        w3_sc_raw = kept("w3_sc_raw", [P, N], U8)
+        w2_sc_raw = kept("w2_sc_raw", [P, PASSES, N], U8)
+        nc.vector.memset(tab_sc[:].bitcast(I32), 0)
+        nc.vector.memset(w3_sc_raw[:].bitcast(I32), 0)
+        nc.vector.memset(w2_sc_raw[:].rearrange("p a c -> p (a c)").bitcast(I32), 0)
+
+        tab = [kept("tab0", [P, T], I32, "stage11"), kept("tab1", [P, T], I32)]
+        w3_raw = kept("w3_raw", [P, PASSES, N], I32, "stage00")
+        w2_raw = kept("w2_raw", [P, PASSES, 2 * N], U8, "stage10")
+        gain_sb = kept("gain_sb", [P, PASSES, PACK], F32)
+        gx_sb = kept("gx_sb", [P, PACK], F32)
+
+        def load_tab(a):
+            nc.sync.dma_start(out=tab[a][:], in_=tab_words[a].rearrange("p t i -> p (t i)").bitcast(I32))
+
+        nc.sync.dma_start(offs_sb[:], offs)
+        nc.sync.dma_start(pos2_sb[:], pos2)
+        nc.sync.dma_start(pos1_sb[:], pos1)
+        nc.sync.dma_start(out=w3_raw[:], in_=w3_words.rearrange("a p c i -> p a (c i)").bitcast(I32))
+        nc.sync.dma_start(out=w2_raw[:].bitcast(I32), in_=w2_words.rearrange("a p c -> p a c").bitcast(I32))
+        load_tab(0)
+        load_tab(1)
+
+        for q in range(4):
+            nc.gpsimd.dma_start(
+                out=tab_sc[32 * q : 32 * q + 8, :].bitcast(I32), in_=tab_scales[:, 4 * q : 4 * q + 4, :].bitcast(I32)
+            )
+        for q in range(4):
+            nc.scalar.dma_start(
+                out=w3_sc_raw[32 * q : 32 * q + 8, :].bitcast(I32), in_=w3_scales[:, 4 * q : 4 * q + 4, :].bitcast(I32)
+            )
+        for q in range(4):
+            nc.gpsimd.dma_start(
+                out=w2_sc_raw[32 * q : 32 * q + 4, :, :].bitcast(I32),
+                in_=w2_scales[:, 4 * q : 4 * q + 4, :].rearrange("a r c -> r a c").bitcast(I32),
+            )
+        nc.scalar.dma_start(out=gain_sb[:], in_=gain.rearrange("(b p t) -> p b t", b=PASSES, t=PACK))
+        nc.scalar.dma_start(out=gx_sb[:], in_=gx.rearrange("(p t) -> p t", t=PACK))
+
+        v_sc = kept("v_sc", [P, S], U8)
+        v = [[kept(f"v{a}{u}", [P, BANK], U32) for u in range(2)] for a in range(PASSES)]
+
+        def gather_words(a, u):
+            nc.vector.tensor_copy(v[a][u][:], tab[a][:].bitcast(U32).indirect(offs_sb[:, 32 * u : 32 * (u + 1)]))
+
+        def v_operand(a, j0, n):
+            u, c = divmod(j0, BANK)
+            return dict(rhs=v[a][u][:, c : c + n].bitcast(FP8X4), rhs_scale=v_sc[4 * a :, j0 : j0 + n])
+
+
+        w3_c = kept("w3_c", [P, PASSES, PACK, P], I32)
+        w3_sc = kept("w3_sc", [P, PACK, P], U8)
+        w2_c = kept("w2_c", [P, PASSES, PACK, P, 2], U8)
+        w2_sc = kept("w2_sc", [P, PASSES, PACK, P], U8)
+        nc.vector.tensor_copy(out=w3_c[:], in_=w3_raw[:].rearrange("p a (m t) -> p a t m", t=PACK))
+        nc.vector.tensor_copy(out=w3_sc[:], in_=w3_sc_raw[:].rearrange("p (m t) -> p t m", t=PACK))
+        nc.vector.tensor_copy(out=w2_c[:], in_=w2_raw[:].rearrange("p a (m t e) -> p a t m e", t=PACK, e=2))
+        nc.vector.tensor_copy(v_sc[:], tab_sc[:].indirect(offs_sb[:]))
+        gather_words(0, 0)
+        gather_words(0, 1)
+        nc.vector.tensor_copy(out=w2_sc[:], in_=w2_sc_raw[:].rearrange("p a (m t) -> p a t m", t=PACK))
+
+        w1_raw = {}
+        for b in range(PASSES):
+            for a in range(PASSES):
+                w1_raw[a, b] = kept(f"w1_raw{a}{b}", [P, PACK, PASS], F32, f"stage{a}{b}")
+                rows = w1[a * PASS : (a + 1) * PASS, b * PASS : (b + 1) * PASS]
+                nc.sync.dma_start(out=w1_raw[a, b][:], in_=rows.rearrange("(p i) c -> p i c", i=PACK))
+
+        skip = [kept(f"skip{t}", [P, S], F32) for t in range(PACK)]
+        skip_ps = {(u, t): psum.tile([P, BANK], F32, name="bank") for u in range(2) for t in range(PACK)}
+
+        def skip_pass(a, u, t):
+            nc.tensor.matmul_mx(
+                out=skip_ps[u, t][:], lhsT=w3_c[:, a, t, :].bitcast(FP8X4), lhsT_scale=w3_sc[4 * a :, t, :],
+                start=(a == 0), stop=(a == PASSES - 1), **v_operand(a, u * BANK, BANK),
+            )
+
+        for u in range(2):
+            for t in range(PACK):
+                skip_pass(0, u, t)
+        for u in range(2):
+            gather_words(1, u)
+            for t in range(PACK):
+                skip_pass(1, u, t)
+                nc.scalar.copy(out=skip[t][:, u * BANK : (u + 1) * BANK], in_=skip_ps[u, t][:])
+
+        w1_c = {}
+        w1_sc = {}
+        w1_bf = {}
+
+        def round_w1(a, b):
+            w1_bf[a, b] = kept(f"w1_bf{a}{b}", [P, PACK, P, PACK], BF16)
+            nc.vector.tensor_copy(
+                out=w1_bf[a, b][:].rearrange("p t m i -> p m t i"),
+                in_=w1_raw[a, b][:].rearrange("p i (m t) -> p m t i", t=PACK),
+            )
+
+        def quantise_w1(a, b):
+            w1_c[a, b] = kept(f"w1_c{a}{b}", [P, PASS], U32)
+            w1_sc[a, b] = kept(f"w1_sc{a}{b}", [P, PASS], U8)
+            nc.vector.quantize_mx(
+                out=w1_c[a, b][:].bitcast(FP8X4), scales=w1_sc[a, b][:],
+                in_=w1_bf[a, b][:].rearrange("p t m i -> p (t m i)"),
+            )
+
+        round_w1(0, 0)
+        round_w1(1, 0)
+        quantise_w1(0, 0)
+        quantise_w1(1, 0)
+
+        steps = [(b, j0) for b in range(PASSES) for j0 in range(0, S, STEP)]
+        mag, logs, h_bf, h_c, h_sc = {}, {}, {}, {}, {}
+        g2 = [kept(f"g2_{t}", [P, S], F32) for t in range(PACK)]
+
+        def first_product(b, j0):
+            mag[b, j0] = ring.tile([P, STEP, PACK], F32, name="mag")
+            for c in range(0, STEP, X_COLS):
+                x = psum.tile([P, BANK], F32, name="bank")
+                for t in range(PACK):
+                    for a in range(PASSES):
+                        nc.tensor.matmul_mx(
+                            out=x[:, t * X_COLS : (t + 1) * X_COLS],
+                            lhsT=w1_c[a, b][:, t * P : (t + 1) * P].bitcast(FP8X4),
+                            lhsT_scale=w1_sc[a, b][:, t * P : (t + 1) * P],
+                            start=(a == 0), stop=(a == PASSES - 1), **v_operand(a, j0 + c, X_COLS),
+                        )
+                nc.scalar.activation(
+                    out=mag[b, j0][:, c : c + X_COLS, :], in_=x[:].rearrange("p (t j) -> p j t", t=PACK), func=ACT.Abs
+                )
+
+        def logarithm(b, j0):
+            logs[b, j0] = ring.tile([P, STEP, PACK], F32, name="logs")
+            nc.scalar.activation(out=logs[b, j0][:], in_=mag[b, j0][:], func=ACT.Ln, bias=1.0)
+
+        def apply_gain(b, j0):
+            h_bf[b, j0] = ring.tile([P, STEP, PACK], BF16, name="h_bf", align_bytes=64)
+            nc.vector.tensor_tensor(
+                out=h_bf[b, j0][:], in0=logs[b, j0][:],
+                in1=gain_sb[:, b : b + 1, :].to_broadcast([P, STEP, PACK]), op=ALU.mult,
+            )
+
+        def quantise_h(b, j0):
+            h_c[b, j0] = kept(f"h_c{b}_{j0}", [P, STEP], U32)
+            h_sc[b, j0] = kept(f"h_sc{b}_{j0}", [P, STEP], U8)
+            nc.vector.quantize_mx(
+                out=h_c[b, j0][:].bitcast(FP8X4), scales=h_sc[b, j0][:],
+                in_=h_bf[b, j0][:].rearrange("p j t -> p (j t)"),
+            )
+
+        mapped = {}
+
+        def second_product(j0):
+            for t0 in range(0, PACK, 2):
+                bank = psum.tile([P, BANK], F32, name="bank")
+                for t in (t0, t0 + 1):
+                    mapped[j0, t] = bank[:, (t - t0) * STEP : (t - t0 + 1) * STEP]
+                    for b in range(PASSES):
+                        nc.tensor.matmul_mx(
+                            out=mapped[j0, t],
+                            lhsT=w2_c[:, b, t, :, :].rearrange("p m e -> p (m e)").bitcast(FP4X4),
+                            lhsT_scale=w2_sc[:, b, t, :],
+                            rhs=h_c[b, j0][:].bitcast(FP8X4), rhs_scale=h_sc[b, j0][:],
+                            start=(b == 0), stop=(b == PASSES - 1),
+                        )
+
+        def cap(j0):
+            for t in range(PACK):
+                nc.vector.tensor_tensor(
+                    out=g2[t][:, j0 : j0 + STEP], in0=mapped[j0, t], in1=skip[t][:, j0 : j0 + STEP], op=ALU.min
+                )
+
+        last = len(steps) - 1
+        for s in range(len(steps) + 4):
+            if s <= last:
+                first_product(*steps[s])
+            if 0 <= s - 1 <= last:
+                logarithm(*steps[s - 1])
+            if 0 <= s - 2 <= last:
+                apply_gain(*steps[s - 2])
+            if s in (1, 2):
+                round_w1(s - 1, 1)
+            if s in (2, 3):
+                quantise_w1(s - 2, 1)
+            if 0 <= s - 4 <= last and steps[s - 4][0] == PASSES - 1:
+                cap(steps[s - 4][1])
+            if 0 <= s - 3 <= last:
+                quantise_h(*steps[s - 3])
+                if steps[s - 3][0] == PASSES - 1:
+                    second_product(steps[s - 3][1])
+
+        y_c = kept("y_c", [P, PAIRS], I32)
+        y_sc = kept("y_sc", [P, PAIRS], U8)
+        out_rows = out_0.rearrange("(p t) m -> p t m", t=PACK)
+        out_words = out_1[0].rearrange("p m t -> p (m t)").bitcast(I32)
+        starts = [sum(PAIR_SLICES[:i]) for i in range(len(PAIR_SLICES))]
+        exit_w, y, y_bf = {}, {}, {}
+
+        def fetch_exit(i):
+            m0, n = starts[i], PAIR_SLICES[i]
+            for t in range(PACK):
+                picked = kept(f"picked{i}{t}", [P, n], F32)
+                nc.vector.tensor_copy(picked[:], g2[t][:].indirect(pos2_sb[:, m0 // 16 : (m0 + n) // 16]))
+                exit_w[i, t] = kept(f"exit_w{i}{t}", [P, n], F32)
+                nc.scalar.activation(out=exit_w[i, t][:], in_=picked[:], func=ACT.Copy, scale=gx_sb[:, t : t + 1])
+
+        def fetch_entry(i):
+            m0, n = starts[i], PAIR_SLICES[i]
+            y[i] = kept(f"y{i}", [P, PACK, n], F32)
+            for t in range(PACK):
+                nc.vector.tensor_tensor(
+                    y[i][:, t, :], g2[t][:].indirect(pos1_sb[:, m0 // 16 : (m0 + n) // 16]), exit_w[i, t][:], ALU.subtract
+                )
+            nc.sync.dma_start(out=out_rows[:, :, m0 : m0 + n], in_=y[i][:])
+            y_bf[i] = kept(f"y_bf{i}", [P, n, PACK], BF16)
+            rounder = nc.vector.tensor_copy if i == len(PAIR_SLICES) - 1 else nc.scalar.copy
+            rounder(out=y_bf[i][:], in_=y[i][:].rearrange("p t m -> p m t"))
+
+        def quantise_y(i):
+            m0, n = starts[i], PAIR_SLICES[i]
+            nc.vector.quantize_mx(
+                out=y_c[:, m0 : m0 + n].bitcast(FP8X4), scales=y_sc[:, m0 : m0 + n],
+                in_=y_bf[i][:].rearrange("p m t -> p (m t)"),
+            )
+            nc.sync.dma_start(out=out_words[:, m0 : m0 + n], in_=y_c[:, m0 : m0 + n])
+
+        fetch_exit(0)
+        for i in range(len(PAIR_SLICES)):
+            if i + 1 < len(PAIR_SLICES):
+                fetch_exit(i + 1)
+            fetch_entry(i)
+            if i > 0:
+                quantise_y(i - 1)
+        quantise_y(len(PAIR_SLICES) - 1)
+        for q in range(4):
+            queue = nc.sync if q % 2 == 0 else nc.scalar
+            queue.dma_start(
+                out=out_2[0, 4 * q : 4 * q + 4, :].bitcast(I32), in_=y_sc[32 * q : 32 * q + 4, :].bitcast(I32)
+            )

@@ -43,16 +43,16 @@ def tile_list_coil_pair_traces_kernel(
         pos1_sb = keep.tile([P, PAIRS // 16], U16, name="pos1_sb")
         pos2_sb = keep.tile([P, PAIRS // 16], U16, name="pos2_sb")
 
-        tab_sc = kept("tab_sc", [P, T], U8, "stage01")
-        w3_sc_raw = kept("w3_sc_raw", [P, N], U8)
+        tab_sc = kept("tab_sc", [P, T], U8, "stage_sc")
+        w3_sc_raw = kept("w3_sc_raw", [P, N], U8, "stage_tab")
         w2_sc_raw = kept("w2_sc_raw", [P, PASSES, N], U8)
         nc.vector.memset(tab_sc[:].bitcast(I32), 0)
-        nc.vector.memset(w3_sc_raw[:].bitcast(I32), 0)
+        nc.gpsimd.memset(w3_sc_raw[:].bitcast(I32), 0)
         nc.vector.memset(w2_sc_raw[:].rearrange("p a c -> p (a c)").bitcast(I32), 0)
 
-        tab = [kept("tab0", [P, T], I32, "stage11"), kept("tab1", [P, T], I32)]
-        w3_raw = kept("w3_raw", [P, PASSES, N], I32, "stage00")
-        w2_raw = kept("w2_raw", [P, PASSES, 2 * N], U8, "stage10")
+        tab = [kept("tab0", [P, T], I32, "stage00"), None]
+        w3_raw = kept("w3_raw", [P, PASSES, N], I32, "stage10")
+        w2_raw = kept("w2_raw", [P, PASSES, 2 * N], U8, "stage01")
         gain_sb = kept("gain_sb", [P, PASSES, PACK], F32)
         gx_sb = kept("gx_sb", [P, PACK], F32)
 
@@ -62,28 +62,26 @@ def tile_list_coil_pair_traces_kernel(
         nc.sync.dma_start(offs_sb[:], offs)
         nc.sync.dma_start(pos2_sb[:], pos2)
         nc.sync.dma_start(pos1_sb[:], pos1)
-        nc.sync.dma_start(out=w3_raw[:], in_=w3_words.rearrange("a p c i -> p a (c i)").bitcast(I32))
-        nc.sync.dma_start(out=w2_raw[:].bitcast(I32), in_=w2_words.rearrange("a p c -> p a c").bitcast(I32))
-        load_tab(0)
-        load_tab(1)
-
         for q in range(4):
-            nc.gpsimd.dma_start(
-                out=tab_sc[32 * q : 32 * q + 8, :].bitcast(I32), in_=tab_scales[:, 4 * q : 4 * q + 4, :].bitcast(I32)
-            )
-        for q in range(4):
-            nc.scalar.dma_start(
+            nc.sync.dma_start(
                 out=w3_sc_raw[32 * q : 32 * q + 8, :].bitcast(I32), in_=w3_scales[:, 4 * q : 4 * q + 4, :].bitcast(I32)
             )
+        load_tab(0)
+        nc.sync.dma_start(out=w3_raw[:], in_=w3_words.rearrange("a p c i -> p a (c i)").bitcast(I32))
+        nc.sync.dma_start(out=w2_raw[:].bitcast(I32), in_=w2_words.rearrange("a p c -> p a c").bitcast(I32))
+        for q in range(4):
+            nc.sync.dma_start(
+                out=tab_sc[32 * q : 32 * q + 8, :].bitcast(I32), in_=tab_scales[:, 4 * q : 4 * q + 4, :].bitcast(I32)
+            )
+        nc.gpsimd.dma_start(out=gain_sb[:], in_=gain.rearrange("(b p t) -> p b t", b=PASSES, t=PACK))
+        nc.gpsimd.dma_start(out=gx_sb[:], in_=gx.rearrange("(p t) -> p t", t=PACK))
         for q in range(4):
             nc.gpsimd.dma_start(
                 out=w2_sc_raw[32 * q : 32 * q + 4, :, :].bitcast(I32),
                 in_=w2_scales[:, 4 * q : 4 * q + 4, :].rearrange("a r c -> r a c").bitcast(I32),
             )
-        nc.scalar.dma_start(out=gain_sb[:], in_=gain.rearrange("(b p t) -> p b t", b=PASSES, t=PACK))
-        nc.scalar.dma_start(out=gx_sb[:], in_=gx.rearrange("(p t) -> p t", t=PACK))
 
-        v_sc = kept("v_sc", [P, S], U8)
+        v_sc = [kept(f"v_sc{u}", [P, BANK], U8) for u in range(2)]
         v = [[kept(f"v{a}{u}", [P, BANK], U32) for u in range(2)] for a in range(PASSES)]
 
         def gather_words(a, u):
@@ -91,27 +89,34 @@ def tile_list_coil_pair_traces_kernel(
 
         def v_operand(a, j0, n):
             u, c = divmod(j0, BANK)
-            return dict(rhs=v[a][u][:, c : c + n].bitcast(FP8X4), rhs_scale=v_sc[4 * a :, j0 : j0 + n])
+            return dict(rhs=v[a][u][:, c : c + n].bitcast(FP8X4), rhs_scale=v_sc[u][4 * a :, c : c + n])
 
 
         w3_c = kept("w3_c", [P, PASSES, PACK, P], I32)
         w3_sc = kept("w3_sc", [P, PACK, P], U8)
-        w2_c = kept("w2_c", [P, PASSES, PACK, P, 2], U8)
         w2_sc = kept("w2_sc", [P, PASSES, PACK, P], U8)
-        nc.vector.tensor_copy(out=w3_c[:], in_=w3_raw[:].rearrange("p a (m t) -> p a t m", t=PACK))
         nc.vector.tensor_copy(out=w3_sc[:], in_=w3_sc_raw[:].rearrange("p (m t) -> p t m", t=PACK))
-        nc.vector.tensor_copy(out=w2_c[:], in_=w2_raw[:].rearrange("p a (m t e) -> p a t m e", t=PACK, e=2))
-        nc.vector.tensor_copy(v_sc[:], tab_sc[:].indirect(offs_sb[:]))
+        tab[1] = kept("tab1", [P, T], I32, "stage_tab")
+        load_tab(1)
+        nc.gpsimd.tensor_copy(out=w2_sc[:], in_=w2_sc_raw[:].rearrange("p a (m t) -> p a t m", t=PACK))
         gather_words(0, 0)
         gather_words(0, 1)
-        nc.vector.tensor_copy(out=w2_sc[:], in_=w2_sc_raw[:].rearrange("p a (m t) -> p a t m", t=PACK))
+        nc.vector.tensor_copy(out=w3_c[:], in_=w3_raw[:].rearrange("p a (m t) -> p a t m", t=PACK))
+        for u in range(2):
+            nc.vector.tensor_copy(v_sc[u][:], tab_sc[:].indirect(offs_sb[:, 32 * u : 32 * (u + 1)]))
+        w2_c = kept("w2_c", [P, PASSES, PACK, P, 2], U8, "stage_sc")
+        nc.vector.tensor_copy(out=w2_c[:], in_=w2_raw[:].rearrange("p a (m t e) -> p a t m e", t=PACK, e=2))
 
         w1_raw = {}
-        for b in range(PASSES):
-            for a in range(PASSES):
-                w1_raw[a, b] = kept(f"w1_raw{a}{b}", [P, PACK, PASS], F32, f"stage{a}{b}")
-                rows = w1[a * PASS : (a + 1) * PASS, b * PASS : (b + 1) * PASS]
-                nc.sync.dma_start(out=w1_raw[a, b][:], in_=rows.rearrange("(p i) c -> p i c", i=PACK))
+
+        def load_w1(a, b, tag):
+            w1_raw[a, b] = kept(f"w1_raw{a}{b}", [P, PACK, PASS], F32, tag)
+            rows = w1[a * PASS : (a + 1) * PASS, b * PASS : (b + 1) * PASS]
+            nc.sync.dma_start(out=w1_raw[a, b][:], in_=rows.rearrange("(p i) c -> p i c", i=PACK))
+
+        load_w1(0, 0, "stage00")
+        load_w1(1, 0, "stage10")
+        load_w1(0, 1, "stage01")
 
         skip = [kept(f"skip{t}", [P, S], F32) for t in range(PACK)]
         skip_ps = {(u, t): psum.tile([P, BANK], F32, name="bank") for u in range(2) for t in range(PACK)}
@@ -131,12 +136,13 @@ def tile_list_coil_pair_traces_kernel(
                 skip_pass(1, u, t)
                 nc.scalar.copy(out=skip[t][:, u * BANK : (u + 1) * BANK], in_=skip_ps[u, t][:])
 
+        load_w1(1, 1, "stage_tab")
         w1_c = {}
         w1_sc = {}
         w1_bf = {}
 
         def round_w1(a, b):
-            w1_bf[a, b] = kept(f"w1_bf{a}{b}", [P, PACK, P, PACK], BF16)
+            w1_bf[a, b] = kept(f"w1_bf{a}{b}", [P, PACK, P, PACK], BF16, f"rounded{2 * b + a}")
             nc.vector.tensor_copy(
                 out=w1_bf[a, b][:].rearrange("p t m i -> p m t i"),
                 in_=w1_raw[a, b][:].rearrange("p i (m t) -> p m t i", t=PACK),
@@ -150,18 +156,22 @@ def tile_list_coil_pair_traces_kernel(
                 in_=w1_bf[a, b][:].rearrange("p t m i -> p (t m i)"),
             )
 
-        round_w1(0, 0)
-        round_w1(1, 0)
-        quantise_w1(0, 0)
-        quantise_w1(1, 0)
+        for b in range(PASSES):
+            round_w1(0, b)
+            round_w1(1, b)
+            quantise_w1(0, b)
+            quantise_w1(1, b)
 
-        steps = [(b, j0) for b in range(PASSES) for j0 in range(0, S, STEP)]
+        steps = [(0, 0, 256), (0, 256, 256), (1, 0, 256), (1, 256, 256), (0, 512, 256), (1, 512, 256), (0, 768, 256), (1, 768, 128), (1, 896, 128)]
         mag, logs, h_bf, h_c, h_sc = {}, {}, {}, {}, {}
         g2 = [kept(f"g2_{t}", [P, S], F32) for t in range(PACK)]
 
-        def first_product(b, j0):
-            mag[b, j0] = ring.tile([P, STEP, PACK], F32, name="mag")
-            for c in range(0, STEP, X_COLS):
+        h_c.update({b: kept(f"h_c{b}", [P, S], U32) for b in range(PASSES)})
+        h_sc.update({b: kept(f"h_sc{b}", [P, S], U8) for b in range(PASSES)})
+
+        def first_product(b, j0, n):
+            mag[b, j0] = ring.tile([P, n, PACK], F32, name="mag")
+            for c in range(0, n, X_COLS):
                 x = psum.tile([P, BANK], F32, name="bank")
                 for t in range(PACK):
                     for a in range(PASSES):
@@ -175,45 +185,44 @@ def tile_list_coil_pair_traces_kernel(
                     out=mag[b, j0][:, c : c + X_COLS, :], in_=x[:].rearrange("p (t j) -> p j t", t=PACK), func=ACT.Abs
                 )
 
-        def logarithm(b, j0):
-            logs[b, j0] = ring.tile([P, STEP, PACK], F32, name="logs")
+        def logarithm(b, j0, n):
+            logs[b, j0] = ring.tile([P, n, PACK], F32, name="logs")
             nc.scalar.activation(out=logs[b, j0][:], in_=mag[b, j0][:], func=ACT.Ln, bias=1.0)
 
-        def apply_gain(b, j0):
-            h_bf[b, j0] = ring.tile([P, STEP, PACK], BF16, name="h_bf", align_bytes=64)
+        def apply_gain(b, j0, n):
+            h_bf[b, j0] = kept(f"h_bf{b}_{j0}", [P, n, PACK], BF16, f"rounded{(3 - len(h_bf)) % 4}")
             nc.vector.tensor_tensor(
                 out=h_bf[b, j0][:], in0=logs[b, j0][:],
-                in1=gain_sb[:, b : b + 1, :].to_broadcast([P, STEP, PACK]), op=ALU.mult,
+                in1=gain_sb[:, b : b + 1, :].to_broadcast([P, n, PACK]), op=ALU.mult,
             )
 
-        def quantise_h(b, j0):
-            h_c[b, j0] = kept(f"h_c{b}_{j0}", [P, STEP], U32)
-            h_sc[b, j0] = kept(f"h_sc{b}_{j0}", [P, STEP], U8)
+        def quantise_h(b, j0, n):
             nc.vector.quantize_mx(
-                out=h_c[b, j0][:].bitcast(FP8X4), scales=h_sc[b, j0][:],
+                out=h_c[b][:, j0 : j0 + n].bitcast(FP8X4), scales=h_sc[b][:, j0 : j0 + n],
                 in_=h_bf[b, j0][:].rearrange("p j t -> p (j t)"),
             )
 
         mapped = {}
 
-        def second_product(j0):
-            for t0 in range(0, PACK, 2):
+        def second_product(j0, n):
+            share = BANK // n
+            for t0 in range(0, PACK, share):
                 bank = psum.tile([P, BANK], F32, name="bank")
-                for t in (t0, t0 + 1):
-                    mapped[j0, t] = bank[:, (t - t0) * STEP : (t - t0 + 1) * STEP]
+                for t in range(t0, min(t0 + share, PACK)):
+                    mapped[j0, t] = bank[:, (t - t0) * n : (t - t0 + 1) * n]
                     for b in range(PASSES):
                         nc.tensor.matmul_mx(
                             out=mapped[j0, t],
                             lhsT=w2_c[:, b, t, :, :].rearrange("p m e -> p (m e)").bitcast(FP4X4),
                             lhsT_scale=w2_sc[:, b, t, :],
-                            rhs=h_c[b, j0][:].bitcast(FP8X4), rhs_scale=h_sc[b, j0][:],
+                            rhs=h_c[b][:, j0 : j0 + n].bitcast(FP8X4), rhs_scale=h_sc[b][:, j0 : j0 + n],
                             start=(b == 0), stop=(b == PASSES - 1),
                         )
 
-        def cap(j0):
+        def cap(j0, n):
             for t in range(PACK):
                 nc.vector.tensor_tensor(
-                    out=g2[t][:, j0 : j0 + STEP], in0=mapped[j0, t], in1=skip[t][:, j0 : j0 + STEP], op=ALU.min
+                    out=g2[t][:, j0 : j0 + n], in0=mapped[j0, t], in1=skip[t][:, j0 : j0 + n], op=ALU.min
                 )
 
         last = len(steps) - 1
@@ -224,16 +233,12 @@ def tile_list_coil_pair_traces_kernel(
                 logarithm(*steps[s - 1])
             if 0 <= s - 2 <= last:
                 apply_gain(*steps[s - 2])
-            if s in (1, 2):
-                round_w1(s - 1, 1)
-            if s in (2, 3):
-                quantise_w1(s - 2, 1)
             if 0 <= s - 4 <= last and steps[s - 4][0] == PASSES - 1:
-                cap(steps[s - 4][1])
+                cap(*steps[s - 4][1:])
             if 0 <= s - 3 <= last:
                 quantise_h(*steps[s - 3])
                 if steps[s - 3][0] == PASSES - 1:
-                    second_product(steps[s - 3][1])
+                    second_product(*steps[s - 3][1:])
 
         y_c = kept("y_c", [P, PAIRS], I32)
         y_sc = kept("y_sc", [P, PAIRS], U8)
@@ -242,20 +247,18 @@ def tile_list_coil_pair_traces_kernel(
         starts = [sum(PAIR_SLICES[:i]) for i in range(len(PAIR_SLICES))]
         exit_w, y, y_bf = {}, {}, {}
 
-        def fetch_exit(i):
-            m0, n = starts[i], PAIR_SLICES[i]
-            for t in range(PACK):
-                picked = kept(f"picked{i}{t}", [P, n], F32)
-                nc.vector.tensor_copy(picked[:], g2[t][:].indirect(pos2_sb[:, m0 // 16 : (m0 + n) // 16]))
-                exit_w[i, t] = kept(f"exit_w{i}{t}", [P, n], F32)
-                nc.scalar.activation(out=exit_w[i, t][:], in_=picked[:], func=ACT.Copy, scale=gx_sb[:, t : t + 1])
+        for t in range(PACK):
+            picked = kept(f"picked{t}", [P, PAIRS], F32)
+            nc.vector.tensor_copy(picked[:], g2[t][:].indirect(pos2_sb[:]))
+            exit_w[t] = kept(f"exit_w{t}", [P, PAIRS], F32)
+            nc.scalar.activation(out=exit_w[t][:], in_=picked[:], func=ACT.Copy, scale=gx_sb[:, t : t + 1])
 
         def fetch_entry(i):
             m0, n = starts[i], PAIR_SLICES[i]
             y[i] = kept(f"y{i}", [P, PACK, n], F32)
             for t in range(PACK):
                 nc.vector.tensor_tensor(
-                    y[i][:, t, :], g2[t][:].indirect(pos1_sb[:, m0 // 16 : (m0 + n) // 16]), exit_w[i, t][:], ALU.subtract
+                    y[i][:, t, :], g2[t][:].indirect(pos1_sb[:, m0 // 16 : (m0 + n) // 16]), exit_w[t][:, m0 : m0 + n], ALU.subtract
                 )
             nc.sync.dma_start(out=out_rows[:, :, m0 : m0 + n], in_=y[i][:])
             y_bf[i] = kept(f"y_bf{i}", [P, n, PACK], BF16)
@@ -270,10 +273,7 @@ def tile_list_coil_pair_traces_kernel(
             )
             nc.sync.dma_start(out=out_words[:, m0 : m0 + n], in_=y_c[:, m0 : m0 + n])
 
-        fetch_exit(0)
         for i in range(len(PAIR_SLICES)):
-            if i + 1 < len(PAIR_SLICES):
-                fetch_exit(i + 1)
             fetch_entry(i)
             if i > 0:
                 quantise_y(i - 1)

@@ -33,8 +33,8 @@ def tile_list_coil_pair_traces_kernel(
     nc = tc.nc
     with ExitStack() as ctx:
         keep = ctx.enter_context(tc.tile_pool(name="keep", bufs=1))
-        ring = ctx.enter_context(tc.tile_pool(name="ring", bufs=3))
-        psum = ctx.enter_context(tc.psum_pool(name="psum", bufs=8))
+        ring = ctx.enter_context(tc.tile_pool(name="ring", bufs=4))
+        psum = ctx.enter_context(tc.psum_pool(name="psum", bufs=4))
 
         def kept(name, shape, dtype, tag=None):
             return keep.tile(shape, dtype, name=name, tag=tag or name, align_bytes=64)
@@ -70,11 +70,11 @@ def tile_list_coil_pair_traces_kernel(
         nc.sync.dma_start(out=w3_raw[:], in_=w3_words.rearrange("a p c i -> p a (c i)").bitcast(I32))
         nc.sync.dma_start(out=w2_raw[:].bitcast(I32), in_=w2_words.rearrange("a p c -> p a c").bitcast(I32))
         for q in range(4):
-            nc.sync.dma_start(
+            nc.gpsimd.dma_start(
                 out=tab_sc[32 * q : 32 * q + 8, :].bitcast(I32), in_=tab_scales[:, 4 * q : 4 * q + 4, :].bitcast(I32)
             )
-        nc.gpsimd.dma_start(out=gain_sb[:], in_=gain.rearrange("(b p t) -> p b t", b=PASSES, t=PACK))
-        nc.gpsimd.dma_start(out=gx_sb[:], in_=gx.rearrange("(p t) -> p t", t=PACK))
+        nc.sync.dma_start(out=gain_sb[:], in_=gain.rearrange("(b p t) -> p b t", b=PASSES, t=PACK))
+        nc.sync.dma_start(out=gx_sb[:], in_=gx.rearrange("(p t) -> p t", t=PACK))
         for q in range(4):
             nc.gpsimd.dma_start(
                 out=w2_sc_raw[32 * q : 32 * q + 4, :, :].bitcast(I32),
@@ -101,11 +101,17 @@ def tile_list_coil_pair_traces_kernel(
         nc.gpsimd.tensor_copy(out=w2_sc[:], in_=w2_sc_raw[:].rearrange("p a (m t) -> p a t m", t=PACK))
         gather_words(0, 0)
         gather_words(0, 1)
-        nc.vector.tensor_copy(out=w3_c[:], in_=w3_raw[:].rearrange("p a (m t) -> p a t m", t=PACK))
+        nc.scalar.copy(
+            out=w3_c[:].bitcast(U32).rearrange("p a t m -> p a m t"),
+            in_=w3_raw[:].bitcast(U32).rearrange("p a (m t) -> p a m t", t=PACK),
+        )
         for u in range(2):
             nc.vector.tensor_copy(v_sc[u][:], tab_sc[:].indirect(offs_sb[:, 32 * u : 32 * (u + 1)]))
-        w2_c = kept("w2_c", [P, PASSES, PACK, P, 2], U8, "stage_sc")
-        nc.vector.tensor_copy(out=w2_c[:], in_=w2_raw[:].rearrange("p a (m t e) -> p a t m e", t=PACK, e=2))
+        w2_c = kept("w2_c", [P, PASSES, PACK, 2 * P], U8)
+        nc.scalar.copy(
+            out=w2_c[:].bitcast(U16).rearrange("p a t m -> p a m t"),
+            in_=w2_raw[:].bitcast(U16).rearrange("p a (m t) -> p a m t", t=PACK),
+        )
 
         w1_raw = {}
 
@@ -114,12 +120,12 @@ def tile_list_coil_pair_traces_kernel(
             rows = w1[a * PASS : (a + 1) * PASS, b * PASS : (b + 1) * PASS]
             nc.sync.dma_start(out=w1_raw[a, b][:], in_=rows.rearrange("(p i) c -> p i c", i=PACK))
 
-        load_w1(0, 0, "stage00")
-        load_w1(1, 0, "stage10")
-        load_w1(0, 1, "stage01")
+        load_w1(0, 0, "stage10")
+        load_w1(1, 0, "stage00")
+        load_w1(0, 1, "stage_sc")
 
         skip = [kept(f"skip{t}", [P, S], F32) for t in range(PACK)]
-        skip_ps = {(u, t): psum.tile([P, BANK], F32, name="bank") for u in range(2) for t in range(PACK)}
+        skip_ps = {(u, t): psum.tile([P, BANK], F32, name=("first", "second")[u]) for u in range(2) for t in range(PACK)}
 
         def skip_pass(a, u, t):
             nc.tensor.matmul_mx(
@@ -144,8 +150,8 @@ def tile_list_coil_pair_traces_kernel(
         def round_w1(a, b):
             w1_bf[a, b] = kept(f"w1_bf{a}{b}", [P, PACK, P, PACK], BF16, f"rounded{2 * b + a}")
             nc.vector.tensor_copy(
-                out=w1_bf[a, b][:].rearrange("p t m i -> p m t i"),
-                in_=w1_raw[a, b][:].rearrange("p i (m t) -> p m t i", t=PACK),
+                out=w1_bf[a, b][:].rearrange("p t m i -> p m i t"),
+                in_=w1_raw[a, b][:].rearrange("p i (m t) -> p m i t", t=PACK),
             )
 
         def quantise_w1(a, b):
@@ -172,14 +178,15 @@ def tile_list_coil_pair_traces_kernel(
         def first_product(b, j0, n):
             mag[b, j0] = ring.tile([P, n, PACK], F32, name="mag")
             for c in range(0, n, X_COLS):
-                x = psum.tile([P, BANK], F32, name="bank")
-                for t in range(PACK):
-                    for a in range(PASSES):
+                x = psum.tile([P, BANK], F32, name="first")
+                for a in range(PASSES):
+                    for t in range(PACK):
                         nc.tensor.matmul_mx(
                             out=x[:, t * X_COLS : (t + 1) * X_COLS],
                             lhsT=w1_c[a, b][:, t * P : (t + 1) * P].bitcast(FP8X4),
                             lhsT_scale=w1_sc[a, b][:, t * P : (t + 1) * P],
-                            start=(a == 0), stop=(a == PASSES - 1), **v_operand(a, j0 + c, X_COLS),
+                            start=(a == 0 and t == 0), stop=(a == PASSES - 1 and t == PACK - 1),
+                            **v_operand(a, j0 + c, X_COLS),
                         )
                 nc.scalar.activation(
                     out=mag[b, j0][:, c : c + X_COLS, :], in_=x[:].rearrange("p (t j) -> p j t", t=PACK), func=ACT.Abs
@@ -202,43 +209,40 @@ def tile_list_coil_pair_traces_kernel(
                 in_=h_bf[b, j0][:].rearrange("p j t -> p (j t)"),
             )
 
+        spans = [(j0, n) for b, j0, n in steps if b == PASSES - 1]
         mapped = {}
 
-        def second_product(j0, n):
+        def second_product(b, j0, n):
             share = BANK // n
-            for t0 in range(0, PACK, share):
-                bank = psum.tile([P, BANK], F32, name="bank")
-                for t in range(t0, min(t0 + share, PACK)):
-                    mapped[j0, t] = bank[:, (t - t0) * n : (t - t0 + 1) * n]
-                    for b in range(PASSES):
-                        nc.tensor.matmul_mx(
-                            out=mapped[j0, t],
-                            lhsT=w2_c[:, b, t, :, :].rearrange("p m e -> p (m e)").bitcast(FP4X4),
-                            lhsT_scale=w2_sc[:, b, t, :],
-                            rhs=h_c[b][:, j0 : j0 + n].bitcast(FP8X4), rhs_scale=h_sc[b][:, j0 : j0 + n],
-                            start=(b == 0), stop=(b == PASSES - 1),
-                        )
-
-        def cap(j0, n):
             for t in range(PACK):
-                nc.vector.tensor_tensor(
-                    out=g2[t][:, j0 : j0 + n], in0=mapped[j0, t], in1=skip[t][:, j0 : j0 + n], op=ALU.min
+                if b == 0 and t % share == 0:
+                    mapped[j0, t // share] = psum.tile([P, share, n], F32, name="second")
+                nc.tensor.matmul_mx(
+                    out=mapped[j0, t // share][:, t % share, :],
+                    lhsT=w2_c[:, b, t, :].bitcast(FP4X4),
+                    lhsT_scale=w2_sc[:, b, t, :],
+                    rhs=h_c[b][:, j0 : j0 + n].bitcast(FP8X4), rhs_scale=h_sc[b][:, j0 : j0 + n],
+                    start=(b == 0 and t % share == 0), stop=(b == PASSES - 1 and t % share == share - 1),
                 )
 
-        last = len(steps) - 1
-        for s in range(len(steps) + 4):
-            if s <= last:
-                first_product(*steps[s])
-            if 0 <= s - 1 <= last:
-                logarithm(*steps[s - 1])
-            if 0 <= s - 2 <= last:
-                apply_gain(*steps[s - 2])
-            if 0 <= s - 4 <= last and steps[s - 4][0] == PASSES - 1:
-                cap(*steps[s - 4][1:])
-            if 0 <= s - 3 <= last:
-                quantise_h(*steps[s - 3])
-                if steps[s - 3][0] == PASSES - 1:
-                    second_product(*steps[s - 3][1:])
+        def cap(j0, n):
+            share = BANK // n
+            for t in range(PACK):
+                nc.vector.tensor_tensor(
+                    out=g2[t][:, j0 : j0 + n], in0=mapped[j0, t // share][:, t % share, :],
+                    in1=skip[t][:, j0 : j0 + n], op=ALU.min,
+                )
+
+        for b, j0, n in steps:
+            first_product(b, j0, n)
+            logarithm(b, j0, n)
+            apply_gain(b, j0, n)
+            quantise_h(b, j0, n)
+            for span in spans:
+                if j0 <= span[0] < j0 + n:
+                    second_product(b, *span)
+            if b == PASSES - 1:
+                cap(j0, n)
 
         y_c = kept("y_c", [P, PAIRS], I32)
         y_sc = kept("y_sc", [P, PAIRS], U8)

@@ -50,6 +50,10 @@ def tile_list_coil_pair_traces_kernel(
         nc.gpsimd.memset(w3_sc_raw[:].bitcast(I32), 0)
         nc.vector.memset(w2_sc_raw[:].rearrange("p a c -> p (a c)").bitcast(I32), 0)
 
+        table_warm = kept("table_warm", [P, 2], F32)
+        nc.gpsimd.memset(table_warm[:, 0:1], 1.0)
+        nc.scalar.activation(out=table_warm[:, 1:2], in_=table_warm[:, 0:1], func=ACT.Ln, bias=1.0)
+
         tab = [kept("tab0", [P, T], I32, "stage00"), None]
         w3_raw = kept("w3_raw", [P, PASSES, N], I32, "stage10")
         w2_raw = kept("w2_raw", [P, PASSES, 2 * N], U8, "stage01")

from contextlib import ExitStack

import concourse.mybir as mybir

K, H, N, T, S, PAIRS = 1024, 1024, 512, 4096, 1024, 512
FLOPS = 2 * S * (K * H + H * N + K * N)

F32 = mybir.dt.float32
BF16 = mybir.dt.bfloat16
I32 = mybir.dt.int32
U32 = mybir.dt.uint32
U16 = mybir.dt.uint16
U8 = mybir.dt.uint8
FP8X4 = mybir.dt.float8_e4m3fn_x4
FP4X4 = mybir.dt.float4_e2m1fn_x4
ACT = mybir.ActivationFunctionType
ALU = mybir.AluOpType

P = 128
PACK = 4
PASS = P * PACK
PASSES = 2
BANK = 512
X_COLS = BANK // PACK
STEP = 256
PAIR_SLICES = (256, 128, 128)


def tile_list_coil_pair_traces_kernel(
    tc, tab_words, tab_scales, offs, w1, gain, w2_words, w2_scales, w3_words, w3_scales, pos1, pos2, gx,
    out_0, out_1, out_2,
):
    nc = tc.nc
    with ExitStack() as ctx:
        keep = ctx.enter_context(tc.tile_pool(name="keep", bufs=1))
        ring = ctx.enter_context(tc.tile_pool(name="ring", bufs=4))
        psum = ctx.enter_context(tc.psum_pool(name="psum", bufs=4))

        def kept(name, shape, dtype, tag=None):
            return keep.tile(shape, dtype, name=name, tag=tag or name, align_bytes=64)

        offs_sb = keep.tile([P, S // 16], U16, name="offs_sb")
        pos1_sb = keep.tile([P, PAIRS // 16], U16, name="pos1_sb")
        pos2_sb = keep.tile([P, PAIRS // 16], U16, name="pos2_sb")

        tab_sc = kept("tab_sc", [P, T], U8, "stage_sc")
        w3_sc_raw = kept("w3_sc_raw", [P, N], U8, "stage_tab")
        w2_sc_raw = kept("w2_sc_raw", [P, PASSES, N], U8)
        nc.vector.memset(tab_sc[:].bitcast(I32), 0)
        nc.gpsimd.memset(w3_sc_raw[:].bitcast(I32), 0)
        nc.vector.memset(w2_sc_raw[:].rearrange("p a c -> p (a c)").bitcast(I32), 0)

        table_warm = kept("table_warm", [P, 2], F32)
        nc.gpsimd.memset(table_warm[:, 0:1], 1.0)
        nc.scalar.activation(out=table_warm[:, 1:2], in_=table_warm[:, 0:1], func=ACT.Ln, bias=1.0)

        tab = [kept("tab0", [P, T], I32, "stage00"), None]
        w3_raw = kept("w3_raw", [P, PASSES, N], I32, "stage10")
        w2_raw = kept("w2_raw", [P, PASSES, 2 * N], U8, "stage01")
        gain_sb = kept("gain_sb", [P, PASSES, PACK], F32)
        gx_sb = kept("gx_sb", [P, PACK], F32)

        def load_tab(a):
            nc.sync.dma_start(out=tab[a][:], in_=tab_words[a].rearrange("p t i -> p (t i)").bitcast(I32))

        nc.sync.dma_start(offs_sb[:], offs)
        nc.sync.dma_start(pos2_sb[:], pos2)
        nc.sync.dma_start(pos1_sb[:], pos1)
        for q in range(4):
            nc.sync.dma_start(
                out=w3_sc_raw[32 * q : 32 * q + 8, :].bitcast(I32), in_=w3_scales[:, 4 * q : 4 * q + 4, :].bitcast(I32)
            )
        load_tab(0)
        nc.sync.dma_start(out=w3_raw[:], in_=w3_words.rearrange("a p c i -> p a (c i)").bitcast(I32))
        nc.sync.dma_start(out=w2_raw[:].bitcast(I32), in_=w2_words.rearrange("a p c -> p a c").bitcast(I32))
        for q in range(4):
            nc.gpsimd.dma_start(
                out=tab_sc[32 * q : 32 * q + 8, :].bitcast(I32), in_=tab_scales[:, 4 * q : 4 * q + 4, :].bitcast(I32)
            )
        nc.sync.dma_start(out=gain_sb[:], in_=gain.rearrange("(b p t) -> p b t", b=PASSES, t=PACK))
        nc.sync.dma_start(out=gx_sb[:], in_=gx.rearrange("(p t) -> p t", t=PACK))
        for q in range(4):
            nc.gpsimd.dma_start(
                out=w2_sc_raw[32 * q : 32 * q + 4, :, :].bitcast(I32),
                in_=w2_scales[:, 4 * q : 4 * q + 4, :].rearrange("a r c -> r a c").bitcast(I32),
            )

        v_sc = [kept(f"v_sc{u}", [P, BANK], U8) for u in range(2)]
        v = [[kept(f"v{a}{u}", [P, BANK], U32) for u in range(2)] for a in range(PASSES)]

        def gather_words(a, u):
            nc.vector.tensor_copy(v[a][u][:], tab[a][:].bitcast(U32).indirect(offs_sb[:, 32 * u : 32 * (u + 1)]))

        def v_operand(a, j0, n):
            u, c = divmod(j0, BANK)
            return dict(rhs=v[a][u][:, c : c + n].bitcast(FP8X4), rhs_scale=v_sc[u][4 * a :, c : c + n])


        w3_c = kept("w3_c", [P, PASSES, PACK, P], I32)
        w3_sc = kept("w3_sc", [P, PACK, P], U8)
        w2_sc = kept("w2_sc", [P, PASSES, PACK, P], U8)
        nc.vector.tensor_copy(out=w3_sc[:], in_=w3_sc_raw[:].rearrange("p (m t) -> p t m", t=PACK))
        tab[1] = kept("tab1", [P, T], I32, "stage_tab")
        load_tab(1)
        nc.gpsimd.tensor_copy(out=w2_sc[:], in_=w2_sc_raw[:].rearrange("p a (m t) -> p a t m", t=PACK))
        gather_words(0, 0)
        gather_words(0, 1)
        nc.scalar.copy(
            out=w3_c[:].bitcast(U32).rearrange("p a t m -> p a m t"),
            in_=w3_raw[:].bitcast(U32).rearrange("p a (m t) -> p a m t", t=PACK),
        )
        for u in range(2):
            nc.vector.tensor_copy(v_sc[u][:], tab_sc[:].indirect(offs_sb[:, 32 * u : 32 * (u + 1)]))
        w2_c = kept("w2_c", [P, PASSES, PACK, 2 * P], U8)
        nc.scalar.copy(
            out=w2_c[:].bitcast(U16).rearrange("p a t m -> p a m t"),
            in_=w2_raw[:].bitcast(U16).rearrange("p a (m t) -> p a m t", t=PACK),
        )

        w1_raw = {}

        def load_w1(a, b, tag):
            w1_raw[a, b] = kept(f"w1_raw{a}{b}", [P, PACK, PASS], F32, tag)
            rows = w1[a * PASS : (a + 1) * PASS, b * PASS : (b + 1) * PASS]
            nc.sync.dma_start(out=w1_raw[a, b][:], in_=rows.rearrange("(p i) c -> p i c", i=PACK))

        load_w1(0, 0, "stage10")
        load_w1(1, 0, "stage00")
        load_w1(0, 1, "stage_sc")

        skip = [kept(f"skip{t}", [P, S], F32) for t in range(PACK)]
        skip_ps = {(u, t): psum.tile([P, BANK], F32, name=("first", "second")[u]) for u in range(2) for t in range(PACK)}

        def skip_pass(a, u, t):
            nc.tensor.matmul_mx(
                out=skip_ps[u, t][:], lhsT=w3_c[:, a, t, :].bitcast(FP8X4), lhsT_scale=w3_sc[4 * a :, t, :],
                start=(a == 0), stop=(a == PASSES - 1), **v_operand(a, u * BANK, BANK),
            )

        for u in range(2):
            for t in range(PACK):
                skip_pass(0, u, t)
        for u in range(2):
            gather_words(1, u)
            for t in range(PACK):
                skip_pass(1, u, t)
                nc.scalar.copy(out=skip[t][:, u * BANK : (u + 1) * BANK], in_=skip_ps[u, t][:])

        load_w1(1, 1, "stage_tab")
        w1_c = {}
        w1_sc = {}
        w1_bf = {}

        def round_w1(a, b):
            w1_bf[a, b] = kept(f"w1_bf{a}{b}", [P, PACK, P, PACK], BF16, f"rounded{2 * b + a}")
            nc.vector.tensor_copy(
                out=w1_bf[a, b][:].rearrange("p t m i -> p m i t"),
                in_=w1_raw[a, b][:].rearrange("p i (m t) -> p m i t", t=PACK),
            )

        def quantise_w1(a, b):
            w1_c[a, b] = kept(f"w1_c{a}{b}", [P, PASS], U32)
            w1_sc[a, b] = kept(f"w1_sc{a}{b}", [P, PASS], U8)
            nc.vector.quantize_mx(
                out=w1_c[a, b][:].bitcast(FP8X4), scales=w1_sc[a, b][:],
                in_=w1_bf[a, b][:].rearrange("p t m i -> p (t m i)"),
            )

        for b in range(PASSES):
            round_w1(0, b)
            round_w1(1, b)
            quantise_w1(0, b)
            quantise_w1(1, b)

        steps = [(0, 0, 256), (0, 256, 256), (1, 0, 256), (1, 256, 256), (0, 512, 256), (1, 512, 256), (0, 768, 256), (1, 768, 128), (1, 896, 128)]
        mag, logs, h_bf, h_c, h_sc = {}, {}, {}, {}, {}
        g2 = [kept(f"g2_{t}", [P, S], F32) for t in range(PACK)]

        h_c.update({b: kept(f"h_c{b}", [P, S], U32) for b in range(PASSES)})
        h_sc.update({b: kept(f"h_sc{b}", [P, S], U8) for b in range(PASSES)})

        def first_product(b, j0, n):
            mag[b, j0] = ring.tile([P, n, PACK], F32, name="mag")
            for c in range(0, n, X_COLS):
                x = psum.tile([P, BANK], F32, name="first")
                for a in range(PASSES):
                    for t in range(PACK):
                        nc.tensor.matmul_mx(
                            out=x[:, t * X_COLS : (t + 1) * X_COLS],
                            lhsT=w1_c[a, b][:, t * P : (t + 1) * P].bitcast(FP8X4),
                            lhsT_scale=w1_sc[a, b][:, t * P : (t + 1) * P],
                            start=(a == 0 and t == 0), stop=(a == PASSES - 1 and t == PACK - 1),
                            **v_operand(a, j0 + c, X_COLS),
                        )
                nc.scalar.activation(
                    out=mag[b, j0][:, c : c + X_COLS, :], in_=x[:].rearrange("p (t j) -> p j t", t=PACK), func=ACT.Abs
                )

        def logarithm(b, j0, n):
            logs[b, j0] = ring.tile([P, n, PACK], F32, name="logs")
            nc.scalar.activation(out=logs[b, j0][:], in_=mag[b, j0][:], func=ACT.Ln, bias=1.0)

        def apply_gain(b, j0, n):
            h_bf[b, j0] = kept(f"h_bf{b}_{j0}", [P, n, PACK], BF16, f"rounded{(3 - len(h_bf)) % 4}")
            nc.vector.tensor_tensor(
                out=h_bf[b, j0][:], in0=logs[b, j0][:],
                in1=gain_sb[:, b : b + 1, :].to_broadcast([P, n, PACK]), op=ALU.mult,
            )

        def quantise_h(b, j0, n):
            nc.vector.quantize_mx(
                out=h_c[b][:, j0 : j0 + n].bitcast(FP8X4), scales=h_sc[b][:, j0 : j0 + n],
                in_=h_bf[b, j0][:].rearrange("p j t -> p (j t)"),
            )

        spans = [(j0, n) for b, j0, n in steps if b == PASSES - 1]
        mapped = {}

        def second_product(b, j0, n):
            share = BANK // n
            for t in range(PACK):
                if b == 0 and t % share == 0:
                    mapped[j0, t // share] = psum.tile([P, share, n], F32, name="second")
                nc.tensor.matmul_mx(
                    out=mapped[j0, t // share][:, t % share, :],
                    lhsT=w2_c[:, b, t, :].bitcast(FP4X4),
                    lhsT_scale=w2_sc[:, b, t, :],
                    rhs=h_c[b][:, j0 : j0 + n].bitcast(FP8X4), rhs_scale=h_sc[b][:, j0 : j0 + n],
                    start=(b == 0 and t % share == 0), stop=(b == PASSES - 1 and t % share == share - 1),
                )

        def cap(j0, n):
            share = BANK // n
            for t in range(PACK):
                nc.vector.tensor_tensor(
                    out=g2[t][:, j0 : j0 + n], in0=mapped[j0, t // share][:, t % share, :],
                    in1=skip[t][:, j0 : j0 + n], op=ALU.min,
                )

        for b, j0, n in steps:
            first_product(b, j0, n)
            logarithm(b, j0, n)
            apply_gain(b, j0, n)
            quantise_h(b, j0, n)
            for span in spans:
                if j0 <= span[0] < j0 + n:
                    second_product(b, *span)
            if b == PASSES - 1:
                cap(j0, n)

        y_c = kept("y_c", [P, PAIRS], I32)
        y_sc = kept("y_sc", [P, PAIRS], U8)
        out_rows = out_0.rearrange("(p t) m -> p t m", t=PACK)
        out_words = out_1[0].rearrange("p m t -> p (m t)").bitcast(I32)
        starts = [sum(PAIR_SLICES[:i]) for i in range(len(PAIR_SLICES))]
        exit_w, y, y_bf = {}, {}, {}

        for t in range(PACK):
            picked = kept(f"picked{t}", [P, PAIRS], F32)
            nc.vector.tensor_copy(picked[:], g2[t][:].indirect(pos2_sb[:]))
            exit_w[t] = kept(f"exit_w{t}", [P, PAIRS], F32)
            nc.scalar.activation(out=exit_w[t][:], in_=picked[:], func=ACT.Copy, scale=gx_sb[:, t : t + 1])

        def fetch_entry(i):
            m0, n = starts[i], PAIR_SLICES[i]
            y[i] = kept(f"y{i}", [P, PACK, n], F32)
            for t in range(PACK):
                nc.vector.tensor_tensor(
                    y[i][:, t, :], g2[t][:].indirect(pos1_sb[:, m0 // 16 : (m0 + n) // 16]), exit_w[t][:, m0 : m0 + n], ALU.subtract
                )
            nc.sync.dma_start(out=out_rows[:, :, m0 : m0 + n], in_=y[i][:])
            y_bf[i] = kept(f"y_bf{i}", [P, n, PACK], BF16)
            rounder = nc.vector.tensor_copy if i == len(PAIR_SLICES) - 1 else nc.scalar.copy
            rounder(out=y_bf[i][:], in_=y[i][:].rearrange("p t m -> p m t"))

        def quantise_y(i):
            m0, n = starts[i], PAIR_SLICES[i]
            nc.vector.quantize_mx(
                out=y_c[:, m0 : m0 + n].bitcast(FP8X4), scales=y_sc[:, m0 : m0 + n],
                in_=y_bf[i][:].rearrange("p m t -> p (m t)"),
            )
            nc.sync.dma_start(out=out_words[:, m0 : m0 + n], in_=y_c[:, m0 : m0 + n])

        for i in range(len(PAIR_SLICES)):
            fetch_entry(i)
            if i > 0:
                quantise_y(i - 1)
        quantise_y(len(PAIR_SLICES) - 1)
        for q in range(4):
            queue = nc.sync if q % 2 == 0 else nc.scalar
            queue.dma_start(
                out=out_2[0, 4 * q : 4 * q + 4, :].bitcast(I32), in_=y_sc[32 * q : 32 * q + 4, :].bitcast(I32)
            )
